import numpy as np
import ml_dtypes


def mxq(x, axis, fmt="e4m3"):
    dtype, down = {"e4m3": (ml_dtypes.float8_e4m3fn, 7), "e5m2": (ml_dtypes.float8_e5m2, 14)}[fmt]
    v = np.moveaxis(np.asarray(x, np.float32).astype(ml_dtypes.bfloat16).astype(np.float64), axis, -1)
    blocks = v.reshape(v.shape[:-1] + (-1, 32))
    amax = np.abs(blocks).max(-1, keepdims=True)
    byte = np.maximum(np.where(amax > 0, np.frexp(amax)[1] - 1 + 127, 0) - down, 1)
    scale = np.exp2(byte - 127.0)
    codes = (blocks / scale).astype(np.float32).astype(dtype).astype(np.float64)
    return np.moveaxis((codes * scale).reshape(v.shape), -1, axis)


WIDE = False


def mx_kscale(k):
    if not WIDE:
        return np.ones(k)
    levels = np.array([10, -10, 5, -5, 0])
    if k % 512:
        return np.exp2(np.random.permutation(np.resize(levels, k // 32))).repeat(32)
    a = np.empty((k // 512, 16))
    for p in range(k // 512):
        a[p, :8] = np.random.permutation(np.resize(levels, 8))
        for g in range(8):
            far = levels[np.abs(levels - a[p, g]) >= 10]
            a[p, g + 8] = far[np.random.randint(len(far))]
    return np.exp2(a.ravel()).repeat(32)


def f64(x):
    return np.asarray(x).astype(np.float64)


def striped(idx):
    return np.tile(idx.reshape(-1, 16).T, (8, 1)).astype(np.uint16)


def unstriped(offs):
    return offs[:16].T.reshape(-1).astype(np.int64)


def striped8(idx):
    return np.concatenate([x.reshape(-1, 16).T for x in idx]).astype(np.uint16)


def runs(offs, k):
    lists = np.stack([offs[16 * r : 16 * r + 16].T.reshape(-1) for r in range(8)]).astype(np.int64)
    return lists[np.arange(k) % 512 // 64]


def pack_weight(w):
    k, n = w.shape
    w = f64(np.asarray(w, np.float32).astype(ml_dtypes.bfloat16)).reshape(k // 32, 32, n)
    amax = np.abs(w).max(1)
    byte = np.clip(np.where(amax > 0, np.frexp(amax)[1] - 1 + 127 - 7, 1), 1, 254)
    scaled = (w * np.exp2(127.0 - byte)[:, None, :]).reshape(k, n).astype(np.float32)
    words = np.ascontiguousarray(scaled.reshape(k // 512, 128, 4, n).transpose(0, 1, 3, 2)).astype(ml_dtypes.float8_e4m3fn).view(np.uint8)
    return words, np.ascontiguousarray(byte.astype(np.uint8).reshape(k // 512, 16, n))


def unpack_weight(words, scales):
    g, p, n, _ = words.shape
    vals = np.ascontiguousarray(words).view(ml_dtypes.float8_e4m3fn).astype(np.float64) * np.repeat(np.exp2(scales.astype(np.float64) - 127.0), 8, axis=1)[..., None]
    return vals.transpose(0, 1, 3, 2).reshape(g * 512, n)


E2M1 = np.array([0.0, 0.5, 1.0, 1.5, 2.0, 3.0, 4.0, 6.0, -0.0, -0.5, -1.0, -1.5, -2.0, -3.0, -4.0, -6.0])


def pack_fp4(w):
    k, n = w.shape
    w = f64(np.asarray(w, np.float32).astype(ml_dtypes.bfloat16)).reshape(k // 32, 32, n)
    amax = np.abs(w).max(1)
    mant, ex = np.frexp(amax / 6.0)
    byte = np.clip(np.where(amax > 0, np.where(mant > 0.5, ex, ex - 1) + 127, 1), 1, 254)
    scaled = (w * np.exp2(127.0 - byte)[:, None, :]).reshape(k, n).astype(np.float32)
    c = np.ascontiguousarray(scaled.reshape(k // 512, 128, 4, n).transpose(0, 1, 3, 2)).astype(ml_dtypes.float4_e2m1fn).view(np.uint8) & 0xF
    words = (c[..., 0::2] | (c[..., 1::2] << 4)).reshape(k // 512, 128, 2 * n)
    return np.ascontiguousarray(words), np.ascontiguousarray(byte.astype(np.uint8).reshape(k // 512, 16, n))


def unpack_fp4(words, scales):
    g, _, n = scales.shape
    words = np.ascontiguousarray(words).reshape(g, 128, n, 2)
    nib = np.empty((g, 128, n, 4), np.uint8)
    nib[..., 0::2] = words & 0xF
    nib[..., 1::2] = words >> 4
    vals = E2M1[nib] * np.repeat(np.exp2(scales.astype(np.float64) - 127.0), 8, axis=1)[..., None]
    return vals.transpose(0, 1, 3, 2).reshape(g * 512, n)


def planes(y):
    n, m = y.shape
    v = y.astype(np.float32).astype(ml_dtypes.bfloat16).astype(np.float64).reshape(n // 32, 32, m)
    top = np.abs(v).max(1)
    byte = np.clip(np.where(top > 0, np.frexp(top)[1] - 1 + 127 - 7, 1), 1, 254)
    codes = (v * np.exp2(127.0 - byte)[:, None, :]).reshape(n, m).astype(np.float32).astype(ml_dtypes.float8_e4m3fn).view(np.uint8)
    words = codes.reshape(n // 512, 128, 4, m).transpose(0, 1, 3, 2)
    return np.ascontiguousarray(words), np.ascontiguousarray(byte.astype(np.uint8).reshape(n // 512, 16, m))


K, T, S, H, C = 512, 2048, 512, 512, 512


def setup_inputs():
    n = np.random.standard_normal
    s = mx_kscale(K)[:, None]
    packed_xT = pack_weight(n((K, T)) * s)
    packed_w1 = pack_fp4(n((K, H)) / np.sqrt(K) / s)
    return {
        "x_words": packed_xT[0],
        "x_scales": packed_xT[1],
        "w1_words": packed_w1[0],
        "w1_scales": packed_w1[1],
        "gs": (np.random.uniform(0.5, 1.5, (K, 1)) / s).astype(np.float32),
        "offs": striped(np.random.permutation(T)[:S]),
        "n1": striped8(np.stack([np.random.permutation(S) for _ in range(8)])),
        "n2": striped8(np.stack([np.random.permutation(S) for _ in range(8)])),
        "n3": striped8(np.stack([np.random.permutation(S) for _ in range(8)])),
        "n4": striped8(np.stack([np.random.permutation(S) for _ in range(8)])),
        "cand": striped(np.random.permutation(T)[:C]),
        "n5": striped8(np.stack([np.random.permutation(S) for _ in range(8)])),
        "n6": striped8(np.stack([np.random.permutation(S) for _ in range(8)])),
    }


def reference(x_words, x_scales, w1_words, w1_scales, gs, offs, n1, n2, n3, n4, cand, n5, n6):
    x_cand = unpack_weight(x_words, x_scales)[:, unstriped(cand)]
    xq = unpack_weight(x_words, x_scales)[:, unstriped(offs)]
    y = unpack_fp4(w1_words, w1_scales).T @ xq
    z = f64(gs) * (0.75 * ((y[np.arange(H)[:, None], runs(n1, H)]) * (y[np.arange(H)[:, None], runs(n2, H)]) - ((y[np.arange(H)[:, None], runs(n3, H)]) * (y[np.arange(H)[:, None], runs(n4, H)]))))
    s = 0.0625 * ((x_cand.T @ mxq(z, 0, "e4m3")))
    out_0 = np.minimum(np.maximum(s, s[np.arange(C)[:, None], runs(n5, C)]), s[np.arange(C)[:, None], runs(n6, C)])
    return (out_0,) + planes(out_0)

@@ -1,0 +1,245 @@
+from contextlib import ExitStack
+
+import concourse.mybir as mybir
+from concourse.masks import make_identity
+
+F32 = mybir.dt.float32
+BF16 = mybir.dt.bfloat16
+I32 = mybir.dt.int32
+U32 = mybir.dt.uint32
+U16 = mybir.dt.uint16
+U8 = mybir.dt.uint8
+FP8X4 = mybir.dt.float8_e4m3fn_x4
+FP4X4 = mybir.dt.float4_e2m1fn_x4
+ALU = mybir.AluOpType
+COPY = mybir.ActivationFunctionType.Copy
+
+P = 128
+PACK = 4
+T = 2048
+S = 512
+BLOCK = 128
+HEAD = 384
+EARLY = 256
+FLOPS = 2 * 2 * 512 * 512 * 512
+
+
+def tile_picked_canddetminmx_none_po_kernel(
+    tc, x_words, x_scales, w1_words, w1_scales, gs, offs, n1, n2, n3, n4, cand, n5, n6, out_0, out_1, out_2
+):
+    nc = tc.nc
+    with ExitStack() as ctx:
+        keep = ctx.enter_context(tc.tile_pool(name="keep", bufs=1))
+        ring = ctx.enter_context(tc.tile_pool(name="ring", bufs=2))
+        psum = ctx.enter_context(tc.psum_pool(name="psum", bufs=1))
+
+        def load_list(name, src):
+            tile = keep.tile([P, S // 16], U16, name=name)
+            nc.sync.dma_start(tile[:], src)
+            return tile
+
+        def load_scale_rows(tile, src):
+            for q in range(4):
+                nc.sync.dma_start(tile[32 * q : 32 * q + 4, :].bitcast(I32), src[0, 4 * q : 4 * q + 4, :].bitcast(I32))
+
+        def entries(lst, lo, hi):
+            return lst[:, lo // 16 : hi // 16]
+
+        x_plane = keep.tile([P, T], U8, align_bytes=64)
+        w_plane = keep.tile([P, S], U8, align_bytes=64, tag="w_plane")
+        nc.gpsimd.memset(x_plane[:].bitcast(I32), 0)
+        nc.gpsimd.memset(w_plane[:].bitcast(I32), 0)
+        warm = keep.tile([P, 2], F32)
+        nc.vector.memset(warm[:, 0:1], 0.0)
+        nc.scalar.activation(warm[:, 1:2], warm[:, 0:1], COPY, scale=0.75)
+
+        offs_t = load_list("offs_t", offs)
+        load_scale_rows(x_plane, x_scales)
+        cand_t = load_list("cand_t", cand)
+        w_raw = keep.tile([P, 2 * S], U8, align_bytes=64)
+        nc.sync.dma_start(w_raw[:].bitcast(I32), w1_words[0].bitcast(I32))
+        x_table = keep.tile([P, T], I32, align_bytes=64)
+        nc.sync.dma_start(x_table[:], x_words[0].rearrange("p n r -> p (n r)").bitcast(I32))
+        load_scale_rows(w_plane, w1_scales)
+        gain = keep.tile([P, PACK], F32)
+        nc.sync.dma_start(gain[:], gs.rearrange("(p t) o -> p (t o)", t=PACK))
+        n1_t = load_list("n1_t", n1)
+        n3_t = load_list("n3_t", n3)
+        n2_t = load_list("n2_t", n2)
+        n4_t = load_list("n4_t", n4)
+        n5_t = load_list("n5_t", n5)
+        n6_t = load_list("n6_t", n6)
+
+        ident = keep.tile([P, P], F32)
+        make_identity(nc, ident[:])
+
+        xq_scales = keep.tile([P, S], U8, align_bytes=64)
+        nc.vector.tensor_copy(xq_scales[:], x_plane[:].indirect(offs_t[:]))
+        cand_scales_raw = keep.tile([P, S], U8, align_bytes=64)
+        nc.vector.tensor_copy(cand_scales_raw[:], x_plane[:].indirect(cand_t[:]))
+        w_codes = keep.tile([P, PACK, BLOCK, 2], U8, align_bytes=64)
+        nc.vector.tensor_copy(
+            w_codes[:].rearrange("p t m b -> p m t b"), w_raw[:].rearrange("p (m t b) -> p m t b", t=PACK, b=2)
+        )
+        xq_codes = keep.tile([P, S], U32, align_bytes=64)
+        nc.vector.tensor_copy(xq_codes[:], x_table[:].bitcast(U32).indirect(offs_t[:]))
+        w_scales = keep.tile([P, PACK, BLOCK], U8, align_bytes=64)
+        nc.vector.tensor_copy(w_scales[:].rearrange("p t m -> p m t"), w_plane[:].rearrange("p (m t) -> p m t", t=PACK))
+        cand_codes_raw = keep.tile([P, S], U32, align_bytes=64, tag="w_plane")
+        nc.vector.tensor_copy(cand_codes_raw[:], x_table[:].bitcast(U32).indirect(cand_t[:]))
+        cand_scales = keep.tile([P, PACK, BLOCK], U8, align_bytes=64)
+        nc.vector.tensor_copy(
+            cand_scales[:].rearrange("p t m -> p m t"), cand_scales_raw[:].rearrange("p (m t) -> p m t", t=PACK)
+        )
+        cand_codes = keep.tile([P, PACK, BLOCK], U32, align_bytes=64)
+        nc.vector.tensor_copy(
+            cand_codes[:].rearrange("p t m -> p m t"), cand_codes_raw[:].rearrange("p (m t) -> p m t", t=PACK)
+        )
+        y_gain, y_pos, y_neg = [], [], []
+        for t in range(PACK):
+            bank = psum.tile([P, S], F32, name="bank%d" % t)
+            nc.tensor.matmul_mx(
+                out=bank[:],
+                lhsT=w_codes[:, t, :, :].rearrange("p m b -> p (m b)").bitcast(FP4X4),
+                lhsT_scale=w_scales[:, t, :],
+                rhs=xq_codes[:].bitcast(FP8X4),
+                rhs_scale=xq_scales[:],
+                start=True,
+                stop=True,
+            )
+            y_gain.append(keep.tile([P, S], F32, name="y_gain%d" % t))
+            y_pos.append(keep.tile([P, S], F32, name="y_pos%d" % t))
+            y_neg.append(keep.tile([P, S], F32, name="y_neg%d" % t))
+            nc.scalar.activation(y_gain[t][:], bank[:], COPY, scale=gain[:, t : t + 1])
+            nc.scalar.activation(y_pos[t][:], bank[:], COPY, scale=0.75)
+            nc.scalar.activation(y_neg[t][:], bank[:], COPY, scale=-0.75)
+
+        z_codes = keep.tile([P, S], U32, align_bytes=64)
+        z_scales = keep.tile([P, S], U8, align_bytes=64)
+        s_bank = [psum.tile([P, S], F32, name="s_bank%d" % t, tag="bank%d" % t) for t in range(PACK)]
+        s_win = [keep.tile([P, S], F32, name="s_win%d" % t) for t in range(PACK)]
+
+        def products(t, lo, hi, first, second, a):
+            c = ring.tile([P, hi - lo], F32, name="c")
+            nc.vector.tensor_copy(a[:], y_gain[t][:].indirect(entries(n1_t, lo, hi)))
+            nc.vector.tensor_copy(c[:], y_gain[t][:].indirect(entries(n3_t, lo, hi)))
+            nc.vector.tensor_tensor(first, y_pos[t][:].indirect(entries(n2_t, lo, hi)), a[:], ALU.mult)
+            nc.vector.tensor_tensor(second, y_neg[t][:].indirect(entries(n4_t, lo, hi)), c[:], ALU.mult)
+
+        def score(lo, hi):
+            for t in range(PACK):
+                nc.tensor.matmul_mx(
+                    out=s_bank[t][:, lo:hi],
+                    lhsT=cand_codes[:, t, :].bitcast(FP8X4),
+                    lhsT_scale=cand_scales[:, t, :],
+                    rhs=z_codes[:, lo:hi].bitcast(FP8X4),
+                    rhs_scale=z_scales[:, lo:hi],
+                    start=True,
+                    stop=True,
+                )
+
+        def leave(lo, hi):
+            for t in range(PACK):
+                nc.scalar.activation(s_win[t][:, lo:hi], s_bank[t][:, lo:hi], COPY, scale=0.0625)
+
+        blocks = HEAD // BLOCK
+        turned = [psum.tile([P, PACK, BLOCK], F32, name="turned%d" % b) for b in range(blocks)]
+        for t in range(PACK):
+            first = ring.tile([P, HEAD], F32, name="first")
+            second = ring.tile([P, HEAD], F32, name="second")
+            products(t, 0, HEAD, first[:], second[:], ring.tile([P, HEAD], F32, name="a"))
+            for b in range(blocks):
+                cols = slice(b * BLOCK, (b + 1) * BLOCK)
+                nc.tensor.matmul(turned[b][:, t, :], first[:, cols], ident[:], start=True, stop=False, is_transpose=True)
+                nc.tensor.matmul(turned[b][:, t, :], second[:, cols], ident[:], start=False, stop=True, is_transpose=True)
+        z_early = keep.tile([P, EARLY * PACK], BF16, align_bytes=64, tag="z_early")
+        z_late = keep.tile([P, BLOCK * PACK], BF16, align_bytes=64, tag="z_late")
+        z_block = [z_early[:, : BLOCK * PACK], z_early[:, BLOCK * PACK :], z_late[:]]
+        for b in range(blocks):
+            pairs = keep.tile([P, 2, P, 2], BF16, name="pairs%d" % b)
+            nc.scalar.copy(pairs[:], turned[b][:].rearrange("j (u e) p -> j u p e", e=2))
+            back = psum.tile([P, 2, BLOCK], F32, name="back%d" % b, tag="turned%d" % b)
+            words = pairs[:].rearrange("j u p e -> j (u p e)").bitcast(F32)
+            for u in range(2):
+                nc.tensor.transpose(back[:, u, :], words[:, u * P : (u + 1) * P], ident[:])
+            nc.scalar.copy(
+                z_block[b].bitcast(F32).rearrange("p (j u) -> p j u", u=2),
+                back[:].rearrange("p u j -> p j u"),
+            )
+
+        def quantize_z(src, lo, hi):
+            nc.vector.quantize_mx(out=z_codes[:, lo:hi].bitcast(FP8X4), scales=z_scales[:, lo:hi], in_=src)
+
+        tail_first = keep.tile([P, PACK, S - HEAD], F32)
+        tail_second = keep.tile([P, PACK, S - HEAD], F32)
+        for t in range(PACK - 1):
+            products(t, HEAD, S, tail_first[:, t, :], tail_second[:, t, :], ring.tile([P, BLOCK], F32, name="a"))
+        quantize_z(z_early[:], 0, EARLY)
+        score(0, EARLY)
+        leave(0, EARLY)
+        a_last = keep.tile([P, BLOCK], F32, align_bytes=64, tag="z_early")
+        products(PACK - 1, HEAD, S, tail_first[:, PACK - 1, :], tail_second[:, PACK - 1, :], a_last)
+        quantize_z(z_late[:], EARLY, HEAD)
+        z_tail = keep.tile([P, (S - HEAD) * PACK], BF16, align_bytes=64, tag="z_late")
+        nc.vector.tensor_tensor(
+            z_tail[:].rearrange("p (c i t) -> p c t i", i=2, t=PACK),
+            tail_first[:].rearrange("p t (c i) -> p c t i", i=2),
+            tail_second[:].rearrange("p t (c i) -> p c t i", i=2),
+            ALU.add,
+        )
+        quantize_z(z_tail[:], HEAD, S)
+        score(EARLY, S)
+        leave(EARLY, S)
+
+        out_rows = out_0.rearrange("(p t) j -> p t j", t=PACK)
+        out_words = out_1[0].rearrange("p n r -> p (n r)").bitcast(I32)
+        o_codes = keep.tile([P, S], I32, align_bytes=64)
+        o_scales = keep.tile([P, S], U8, align_bytes=64)
+
+        def quantize_out(src, lo, hi):
+            nc.vector.quantize_mx(out=o_codes[:, lo:hi].bitcast(FP8X4), scales=o_scales[:, lo:hi], in_=src)
+
+        def fetch(lst, name, t, lo, hi):
+            got = ring.tile([P, hi - lo], F32, name=name)
+            nc.vector.tensor_copy(got[:], s_win[t][:].indirect(entries(lst, lo, hi)))
+            return got
+
+        pieces = ((0, HEAD), (HEAD, S))
+        results = [keep.tile([P, PACK, hi - lo], F32, name="result%d" % lo) for lo, hi in pieces]
+        rounded = [keep.tile([P, (hi - lo) * PACK], BF16, name="rounded%d" % lo, align_bytes=64) for lo, hi in pieces]
+        steps = [(i, t) for i in range(2) for t in range(PACK)]
+
+        def finish(i, t, larger, c):
+            lo, hi = pieces[i]
+            nc.vector.tensor_tensor(results[i][:, t, :], larger[:], c[:], ALU.min)
+            nc.sync.dma_start(out_rows[:, t, lo:hi], results[i][:, t, :])
+            if (i, t) == (0, PACK - 1):
+                nc.scalar.copy(
+                    rounded[0][:].rearrange("p (c i t) -> p c t i", i=2, t=PACK),
+                    results[0][:].rearrange("p t (c i) -> p c t i", i=2),
+                )
+
+        pending = None
+        for i, t in steps:
+            lo, hi = pieces[i]
+            a = fetch(n5_t, "a", t, lo, hi)
+            if pending is not None:
+                finish(*pending)
+            c = fetch(n6_t, "c", t, lo, hi)
+            larger = ring.tile([P, hi - lo], F32, name="larger")
+            nc.vector.tensor_tensor(larger[:], s_win[t][:, lo:hi], a[:], ALU.max)
+            pending = (i, t, larger, c)
+            if (i, t) == (1, PACK - 1):
+                quantize_out(rounded[0][:, : 256 * PACK], 0, 256)
+                quantize_out(rounded[0][:, 256 * PACK :], 256, HEAD)
+                nc.sync.dma_start(out_words[:, :HEAD], o_codes[:, :HEAD])
+        finish(*pending)
+        nc.vector.tensor_copy(
+            rounded[1][:].rearrange("p (c i t) -> p c t i", i=2, t=PACK),
+            results[1][:].rearrange("p t (c i) -> p c t i", i=2),
+        )
+        quantize_out(rounded[1][:], HEAD, S)
+        nc.sync.dma_start(out_words[:, HEAD:], o_codes[:, HEAD:])
+        for q in range(4):
+            queue = nc.scalar if q % 2 else nc.sync
+            queue.dma_start(out_2[0, 4 * q : 4 * q + 4, :].bitcast(I32), o_scales[32 * q : 32 * q + 4, :].bitcast(I32))

@@ -13,6 +13,7 @@ FP8X4 = mybir.dt.float8_e4m3fn_x4
 FP4X4 = mybir.dt.float4_e2m1fn_x4
 ALU = mybir.AluOpType
 COPY = mybir.ActivationFunctionType.Copy
+RELU = mybir.ActivationFunctionType.Relu
 
 P = 128
 PACK = 4
@@ -31,6 +32,7 @@ def tile_picked_canddetminmx_none_po_kernel(
     with ExitStack() as ctx:
         keep = ctx.enter_context(tc.tile_pool(name="keep", bufs=1))
         ring = ctx.enter_context(tc.tile_pool(name="ring", bufs=2))
+        deep = ctx.enter_context(tc.tile_pool(name="deep", bufs=3))
         psum = ctx.enter_context(tc.psum_pool(name="psum", bufs=1))
 
         def load_list(name, src):
@@ -78,22 +80,19 @@ def tile_picked_canddetminmx_none_po_kernel(
         cand_scales_raw = keep.tile([P, S], U8, align_bytes=64)
         nc.vector.tensor_copy(cand_scales_raw[:], x_plane[:].indirect(cand_t[:]))
         w_codes = keep.tile([P, PACK, BLOCK, 2], U8, align_bytes=64)
-        nc.vector.tensor_copy(
-            w_codes[:].rearrange("p t m b -> p m t b"), w_raw[:].rearrange("p (m t b) -> p m t b", t=PACK, b=2)
-        )
+        nc.vector.tensor_copy(w_codes[:], w_raw[:].rearrange("p (m t b) -> p t m b", t=PACK, b=2))
         xq_codes = keep.tile([P, S], U32, align_bytes=64)
         nc.vector.tensor_copy(xq_codes[:], x_table[:].bitcast(U32).indirect(offs_t[:]))
         w_scales = keep.tile([P, PACK, BLOCK], U8, align_bytes=64)
-        nc.vector.tensor_copy(w_scales[:].rearrange("p t m -> p m t"), w_plane[:].rearrange("p (m t) -> p m t", t=PACK))
+        nc.vector.tensor_copy(w_scales[:], w_plane[:].rearrange("p (m t) -> p t m", t=PACK))
         cand_codes_raw = keep.tile([P, S], U32, align_bytes=64, tag="w_plane")
         nc.vector.tensor_copy(cand_codes_raw[:], x_table[:].bitcast(U32).indirect(cand_t[:]))
         cand_scales = keep.tile([P, PACK, BLOCK], U8, align_bytes=64)
-        nc.vector.tensor_copy(
-            cand_scales[:].rearrange("p t m -> p m t"), cand_scales_raw[:].rearrange("p (m t) -> p m t", t=PACK)
-        )
+        nc.vector.tensor_copy(cand_scales[:], cand_scales_raw[:].rearrange("p (m t) -> p t m", t=PACK))
         cand_codes = keep.tile([P, PACK, BLOCK], U32, align_bytes=64)
         nc.vector.tensor_copy(
-            cand_codes[:].rearrange("p t m -> p m t"), cand_codes_raw[:].rearrange("p (m t) -> p m t", t=PACK)
+            cand_codes[:].rearrange("p t (c i) -> p c t i", i=4),
+            cand_codes_raw[:].rearrange("p (c i t) -> p c t i", i=4, t=PACK),
         )
         y_gain, y_pos, y_neg = [], [], []
         for t in range(PACK):
@@ -119,12 +118,13 @@ def tile_picked_canddetminmx_none_po_kernel(
         s_bank = [psum.tile([P, S], F32, name="s_bank%d" % t, tag="bank%d" % t) for t in range(PACK)]
         s_win = [keep.tile([P, S], F32, name="s_win%d" % t) for t in range(PACK)]
 
-        def products(t, lo, hi, first, second, a):
-            c = ring.tile([P, hi - lo], F32, name="c")
-            nc.vector.tensor_copy(a[:], y_gain[t][:].indirect(entries(n1_t, lo, hi)))
-            nc.vector.tensor_copy(c[:], y_gain[t][:].indirect(entries(n3_t, lo, hi)))
-            nc.vector.tensor_tensor(first, y_pos[t][:].indirect(entries(n2_t, lo, hi)), a[:], ALU.mult)
-            nc.vector.tensor_tensor(second, y_neg[t][:].indirect(entries(n4_t, lo, hi)), c[:], ALU.mult)
+        s_plain = [keep.tile([P, S], F32, name="s_plain%d" % t) for t in range(PACK)]
+
+        def products(t, lo, hi, first, second, a, c):
+            nc.vector.tensor_copy(a, y_gain[t][:].indirect(entries(n1_t, lo, hi)))
+            nc.vector.tensor_copy(c, y_gain[t][:].indirect(entries(n3_t, lo, hi)))
+            nc.vector.tensor_tensor(first, y_pos[t][:].indirect(entries(n2_t, lo, hi)), a, ALU.mult)
+            nc.vector.tensor_tensor(second, y_neg[t][:].indirect(entries(n4_t, lo, hi)), c, ALU.mult)
 
         def score(lo, hi):
             for t in range(PACK):
@@ -143,11 +143,13 @@ def tile_picked_canddetminmx_none_po_kernel(
                 nc.scalar.activation(s_win[t][:, lo:hi], s_bank[t][:, lo:hi], COPY, scale=0.0625)
 
         blocks = HEAD // BLOCK
+        factor_a = keep.tile([P, HEAD], F32)
+        factor_c = keep.tile([P, HEAD], F32)
         turned = [psum.tile([P, PACK, BLOCK], F32, name="turned%d" % b) for b in range(blocks)]
         for t in range(PACK):
             first = ring.tile([P, HEAD], F32, name="first")
             second = ring.tile([P, HEAD], F32, name="second")
-            products(t, 0, HEAD, first[:], second[:], ring.tile([P, HEAD], F32, name="a"))
+            products(t, 0, HEAD, first[:], second[:], factor_a[:], factor_c[:])
             for b in range(blocks):
                 cols = slice(b * BLOCK, (b + 1) * BLOCK)
                 nc.tensor.matmul(turned[b][:, t, :], first[:, cols], ident[:], start=True, stop=False, is_transpose=True)
@@ -173,12 +175,15 @@ def tile_picked_canddetminmx_none_po_kernel(
         tail_first = keep.tile([P, PACK, S - HEAD], F32)
         tail_second = keep.tile([P, PACK, S - HEAD], F32)
         for t in range(PACK - 1):
-            products(t, HEAD, S, tail_first[:, t, :], tail_second[:, t, :], ring.tile([P, BLOCK], F32, name="a"))
+            cols = slice(t * BLOCK, (t + 1) * BLOCK)
+            products(t, HEAD, S, tail_first[:, t, :], tail_second[:, t, :], factor_a[:, cols], factor_c[:, cols])
         quantize_z(z_early[:], 0, EARLY)
         score(0, EARLY)
         leave(0, EARLY)
-        a_last = keep.tile([P, BLOCK], F32, align_bytes=64, tag="z_early")
-        products(PACK - 1, HEAD, S, tail_first[:, PACK - 1, :], tail_second[:, PACK - 1, :], a_last)
+        for t in range(2):
+            nc.scalar.activation(s_plain[t][:, :EARLY], s_bank[t][:, :EARLY], COPY, scale=0.0625)
+        last = keep.tile([P, 2, BLOCK], F32, align_bytes=64, tag="z_early")
+        products(PACK - 1, HEAD, S, tail_first[:, PACK - 1, :], tail_second[:, PACK - 1, :], last[:, 0, :], last[:, 1, :])
         quantize_z(z_late[:], EARLY, HEAD)
         z_tail = keep.tile([P, (S - HEAD) * PACK], BF16, align_bytes=64, tag="z_late")
         nc.vector.tensor_tensor(
@@ -189,7 +194,10 @@ def tile_picked_canddetminmx_none_po_kernel(
         )
         quantize_z(z_tail[:], HEAD, S)
         score(EARLY, S)
-        leave(EARLY, S)
+        for t in range(PACK):
+            nc.scalar.activation(s_win[t][:, EARLY:], s_bank[t][:, EARLY:], COPY, scale=0.0625)
+            lo = EARLY if t < 2 else 0
+            nc.scalar.activation(s_plain[t][:, lo:], s_bank[t][:, lo:], COPY, scale=0.0625)
 
         out_rows = out_0.rearrange("(p t) j -> p t j", t=PACK)
         out_words = out_1[0].rearrange("p n r -> p (n r)").bitcast(I32)
@@ -199,47 +207,74 @@ def tile_picked_canddetminmx_none_po_kernel(
         def quantize_out(src, lo, hi):
             nc.vector.quantize_mx(out=o_codes[:, lo:hi].bitcast(FP8X4), scales=o_scales[:, lo:hi], in_=src)
 
-        def fetch(lst, name, t, lo, hi):
-            got = ring.tile([P, hi - lo], F32, name=name)
-            nc.vector.tensor_copy(got[:], s_win[t][:].indirect(entries(lst, lo, hi)))
-            return got
+        def fetch(t, lo, hi, got):
+            nc.vector.tensor_copy(got, s_win[t][:].indirect(entries(n6_t, lo, hi)))
+
+        across = [psum.tile([P, PACK, BLOCK], F32, name="across%d" % t, tag="turned%d" % t) for t in range(PACK)]
+        for t in range(PACK):
+            for b in range(PACK):
+                cols = slice(b * BLOCK, (b + 1) * BLOCK)
+                nc.tensor.matmul(across[t][:, b, :], s_win[t][:, cols], ident[:], start=b == 0, stop=False, is_transpose=True)
+
+        def larger_of(t):
+            excess = keep.tile([P, S], F32, name="excess%d" % t)
+            for lo in (0, S // 2):
+                cols = slice(lo, lo + S // 2)
+                nc.vector.tensor_tensor(
+                    excess[:, cols], s_win[t][:].indirect(entries(n5_t, lo, lo + S // 2)), s_plain[t][:, cols], ALU.subtract
+                )
+            rise = ring.tile([P, S], F32, name="rise")
+            nc.scalar.activation(rise[:], excess[:], RELU)
+            for b in range(PACK):
+                cols = slice(b * BLOCK, (b + 1) * BLOCK)
+                nc.tensor.matmul(
+                    across[t][:, b, :], rise[:, cols], ident[:], start=False, stop=b == PACK - 1, is_transpose=True
+                )
+            staged = ring.tile([P, PACK, BLOCK], F32, name="staged")
+            nc.scalar.copy(staged[:], across[t][:])
+            larger = psum.tile([P, S], F32, name="larger%d" % t, tag="bank%d" % t)
+            for b in range(PACK):
+                nc.tensor.transpose(larger[:, b * BLOCK : (b + 1) * BLOCK], staged[:, b, :], ident[:])
+            return larger
 
         pieces = ((0, HEAD), (HEAD, S))
-        results = [keep.tile([P, PACK, hi - lo], F32, name="result%d" % lo) for lo, hi in pieces]
+        spare = keep.tile([P, HEAD], F32)
+        result_head = keep.tile([P, PACK, HEAD], F32)
+        result_tail = keep.tile([P, PACK, BLOCK], F32)
         rounded = [keep.tile([P, (hi - lo) * PACK], BF16, name="rounded%d" % lo, align_bytes=64) for lo, hi in pieces]
-        steps = [(i, t) for i in range(2) for t in range(PACK)]
+        got_head = [spare[:], s_plain[2][:, :HEAD], spare[:], s_plain[3][:, :HEAD]]
+        got_tail = [s_plain[2][:, :BLOCK]] + [s_plain[3][:, k * BLOCK : (k + 1) * BLOCK] for k in range(3)]
 
-        def finish(i, t, larger, c):
-            lo, hi = pieces[i]
-            nc.vector.tensor_tensor(results[i][:, t, :], larger[:], c[:], ALU.min)
-            nc.sync.dma_start(out_rows[:, t, lo:hi], results[i][:, t, :])
-            if (i, t) == (0, PACK - 1):
-                nc.scalar.copy(
-                    rounded[0][:].rearrange("p (c i t) -> p c t i", i=2, t=PACK),
-                    results[0][:].rearrange("p t (c i) -> p c t i", i=2),
-                )
-
-        pending = None
-        for i, t in steps:
-            lo, hi = pieces[i]
-            a = fetch(n5_t, "a", t, lo, hi)
-            if pending is not None:
-                finish(*pending)
-            c = fetch(n6_t, "c", t, lo, hi)
-            larger = ring.tile([P, hi - lo], F32, name="larger")
-            nc.vector.tensor_tensor(larger[:], s_win[t][:, lo:hi], a[:], ALU.max)
-            pending = (i, t, larger, c)
-            if (i, t) == (1, PACK - 1):
-                quantize_out(rounded[0][:, : 256 * PACK], 0, 256)
-                quantize_out(rounded[0][:, 256 * PACK :], 256, HEAD)
-                nc.sync.dma_start(out_words[:, :HEAD], o_codes[:, :HEAD])
-        finish(*pending)
+        fetch(0, 0, HEAD, got_head[0])
+        larger = [larger_of(t) for t in range(PACK)]
+        fetch(1, 0, HEAD, got_head[1])
+        for t in range(PACK):
+            nc.vector.tensor_tensor(result_head[:, t, :], larger[t][:, :HEAD], got_head[t], ALU.min)
+            nc.sync.dma_start(out_rows[:, t, :HEAD], result_head[:, t, :])
+            if t + 2 < PACK:
+                fetch(t + 2, 0, HEAD, got_head[t + 2])
+        for a, b in ((0, EARLY), (EARLY, HEAD)):
+            nc.scalar.copy(
+                rounded[0][:, a * PACK : b * PACK].rearrange("p (c i t) -> p c t i", i=2, t=PACK),
+                result_head[:, :, a:b].rearrange("p t (c i) -> p c t i", i=2),
+            )
+        fetch(0, HEAD, S, got_tail[0])
+        for t in range(PACK):
+            if t + 1 < PACK:
+                fetch(t + 1, HEAD, S, got_tail[t + 1])
+            else:
+                quantize_out(rounded[0][:, : EARLY * PACK], 0, EARLY)
+            nc.vector.tensor_tensor(result_tail[:, t, :], larger[t][:, HEAD:], got_tail[t], ALU.min)
+            if t % 2:
+                nc.sync.dma_start(out_rows[:, t - 1 : t + 1, HEAD:], result_tail[:, t - 1 : t + 1, :])
         nc.vector.tensor_copy(
             rounded[1][:].rearrange("p (c i t) -> p c t i", i=2, t=PACK),
-            results[1][:].rearrange("p t (c i) -> p c t i", i=2),
+            result_tail[:].rearrange("p t (c i) -> p c t i", i=2),
         )
+        quantize_out(rounded[0][:, EARLY * PACK :], EARLY, HEAD)
         quantize_out(rounded[1][:], HEAD, S)
-        nc.sync.dma_start(out_words[:, HEAD:], o_codes[:, HEAD:])
+        nc.sync.dma_start(out_words[:, :EARLY], o_codes[:, :EARLY])
+        nc.sync.dma_start(out_words[:, EARLY:], o_codes[:, EARLY:])
         for q in range(4):
             queue = nc.scalar if q % 2 else nc.sync
             queue.dma_start(out_2[0, 4 * q : 4 * q + 4, :].bitcast(I32), o_scales[32 * q : 32 * q + 4, :].bitcast(I32))

@@ -51,9 +51,6 @@ def tile_picked_canddetminmx_none_po_kernel(
         w_plane = keep.tile([P, S], U8, align_bytes=64, tag="w_plane")
         nc.gpsimd.memset(x_plane[:].bitcast(I32), 0)
         nc.gpsimd.memset(w_plane[:].bitcast(I32), 0)
-        warm = keep.tile([P, 2], F32)
-        nc.vector.memset(warm[:, 0:1], 0.0)
-        nc.scalar.activation(warm[:, 1:2], warm[:, 0:1], COPY, scale=0.75)
 
         offs_t = load_list("offs_t", offs)
         load_scale_rows(x_plane, x_scales)
@@ -79,57 +76,59 @@ def tile_picked_canddetminmx_none_po_kernel(
         nc.vector.tensor_copy(xq_scales[:], x_plane[:].indirect(offs_t[:]))
         cand_scales_raw = keep.tile([P, S], U8, align_bytes=64)
         nc.vector.tensor_copy(cand_scales_raw[:], x_plane[:].indirect(cand_t[:]))
-        w_codes = keep.tile([P, PACK, BLOCK, 2], U8, align_bytes=64)
-        nc.vector.tensor_copy(w_codes[:], w_raw[:].rearrange("p (m t b) -> p t m b", t=PACK, b=2))
+        w_codes = [keep.tile([P, BLOCK, 2], U8, align_bytes=64, name="w_codes%d" % t) for t in range(PACK)]
+        w_scales = [keep.tile([P, BLOCK], U8, align_bytes=64, name="w_scales%d" % t) for t in range(PACK)]
+        for t in range(PACK):
+            nc.gpsimd.tensor_copy(w_codes[t][:], w_raw[:].rearrange("p (m t b) -> p t m b", t=PACK, b=2)[:, t, :, :])
+            nc.gpsimd.tensor_copy(w_scales[t][:], w_plane[:].rearrange("p (m t) -> p t m", t=PACK)[:, t, :])
         xq_codes = keep.tile([P, S], U32, align_bytes=64)
-        nc.vector.tensor_copy(xq_codes[:], x_table[:].bitcast(U32).indirect(offs_t[:]))
-        w_scales = keep.tile([P, PACK, BLOCK], U8, align_bytes=64)
-        nc.vector.tensor_copy(w_scales[:], w_plane[:].rearrange("p (m t) -> p t m", t=PACK))
-        cand_codes_raw = keep.tile([P, S], U32, align_bytes=64, tag="w_plane")
-        nc.vector.tensor_copy(cand_codes_raw[:], x_table[:].bitcast(U32).indirect(cand_t[:]))
+        for lo in (0, S // 2):
+            nc.vector.tensor_copy(
+                xq_codes[:, lo : lo + S // 2], x_table[:].bitcast(U32).indirect(entries(offs_t, lo, lo + S // 2))
+            )
+        cand_codes = keep.tile([P, PACK, BLOCK], U32, align_bytes=64)
+        nc.vector.tensor_copy(cand_codes[:].rearrange("p t m -> p m t"), x_table[:].bitcast(U32).indirect(cand_t[:]))
         cand_scales = keep.tile([P, PACK, BLOCK], U8, align_bytes=64)
         nc.vector.tensor_copy(cand_scales[:], cand_scales_raw[:].rearrange("p (m t) -> p t m", t=PACK))
-        cand_codes = keep.tile([P, PACK, BLOCK], U32, align_bytes=64)
-        nc.vector.tensor_copy(
-            cand_codes[:].rearrange("p t (c i) -> p c t i", i=4),
-            cand_codes_raw[:].rearrange("p (c i t) -> p c t i", i=4, t=PACK),
-        )
-        y_gain, y_pos, y_neg = [], [], []
+
+        y_gain = [keep.tile([P, S], F32, name="y_gain%d" % t) for t in range(PACK)]
+        y_pos = [keep.tile([P, S], F32, name="y_pos%d" % t) for t in range(PACK)]
+        y_neg = [keep.tile([P, S], F32, name="y_neg%d" % t) for t in range(PACK)]
         for t in range(PACK):
-            bank = psum.tile([P, S], F32, name="bank%d" % t)
-            nc.tensor.matmul_mx(
-                out=bank[:],
-                lhsT=w_codes[:, t, :, :].rearrange("p m b -> p (m b)").bitcast(FP4X4),
-                lhsT_scale=w_scales[:, t, :],
-                rhs=xq_codes[:].bitcast(FP8X4),
-                rhs_scale=xq_scales[:],
-                start=True,
-                stop=True,
-            )
-            y_gain.append(keep.tile([P, S], F32, name="y_gain%d" % t))
-            y_pos.append(keep.tile([P, S], F32, name="y_pos%d" % t))
-            y_neg.append(keep.tile([P, S], F32, name="y_neg%d" % t))
-            nc.scalar.activation(y_gain[t][:], bank[:], COPY, scale=gain[:, t : t + 1])
-            nc.scalar.activation(y_pos[t][:], bank[:], COPY, scale=0.75)
-            nc.scalar.activation(y_neg[t][:], bank[:], COPY, scale=-0.75)
+            parts = ((0, S // 2, "turned3"), (S // 2, S, "bank0")) if t == 0 else ((0, S, "bank%d" % t),)
+            banks = []
+            for lo, hi, tag in parts:
+                bank = psum.tile([P, hi - lo], F32, name="y_bank", tag=tag)
+                banks.append(bank)
+                nc.tensor.matmul_mx(
+                    out=bank[:],
+                    lhsT=w_codes[t][:].rearrange("p m b -> p (m b)").bitcast(FP4X4),
+                    lhsT_scale=w_scales[t][:],
+                    rhs=xq_codes[:, lo:hi].bitcast(FP8X4),
+                    rhs_scale=xq_scales[:, lo:hi],
+                    start=True,
+                    stop=True,
+                )
+            for window, scale in ((y_pos[t], 0.75), (y_neg[t], -0.75), (y_gain[t], gain[:, t : t + 1])):
+                for (lo, hi, tag), bank in zip(parts, banks):
+                    nc.scalar.activation(window[:, lo:hi], bank[:], COPY, scale=scale)
 
         z_codes = keep.tile([P, S], U32, align_bytes=64)
         z_scales = keep.tile([P, S], U8, align_bytes=64)
         s_bank = [psum.tile([P, S], F32, name="s_bank%d" % t, tag="bank%d" % t) for t in range(PACK)]
         s_win = [keep.tile([P, S], F32, name="s_win%d" % t) for t in range(PACK)]
 
-        s_plain = [keep.tile([P, S], F32, name="s_plain%d" % t) for t in range(PACK)]
 
         def products(t, lo, hi, first, second, a, c):
-            nc.vector.tensor_copy(a, y_gain[t][:].indirect(entries(n1_t, lo, hi)))
-            nc.vector.tensor_copy(c, y_gain[t][:].indirect(entries(n3_t, lo, hi)))
-            nc.vector.tensor_tensor(first, y_pos[t][:].indirect(entries(n2_t, lo, hi)), a, ALU.mult)
-            nc.vector.tensor_tensor(second, y_neg[t][:].indirect(entries(n4_t, lo, hi)), c, ALU.mult)
+            nc.vector.tensor_copy(a, y_pos[t][:].indirect(entries(n1_t, lo, hi)))
+            nc.vector.tensor_copy(c, y_neg[t][:].indirect(entries(n3_t, lo, hi)))
+            nc.vector.tensor_tensor(first, y_gain[t][:].indirect(entries(n2_t, lo, hi)), a, ALU.mult)
+            nc.vector.tensor_tensor(second, y_gain[t][:].indirect(entries(n4_t, lo, hi)), c, ALU.mult)
 
-        def score(lo, hi):
-            for t in range(PACK):
+        def score(lo, hi, tiles=range(PACK), bank=None):
+            for t in tiles:
                 nc.tensor.matmul_mx(
-                    out=s_bank[t][:, lo:hi],
+                    out=(s_bank[t] if bank is None else bank)[:, lo:hi],
                     lhsT=cand_codes[:, t, :].bitcast(FP8X4),
                     lhsT_scale=cand_scales[:, t, :],
                     rhs=z_codes[:, lo:hi].bitcast(FP8X4),
@@ -138,9 +137,8 @@ def tile_picked_canddetminmx_none_po_kernel(
                     stop=True,
                 )
 
-        def leave(lo, hi):
-            for t in range(PACK):
-                nc.scalar.activation(s_win[t][:, lo:hi], s_bank[t][:, lo:hi], COPY, scale=0.0625)
+        def leave(tile, bank, lo, hi):
+            nc.scalar.activation(tile[:, lo:hi], bank[:, lo:hi], COPY, scale=0.0625)
 
         blocks = HEAD // BLOCK
         factor_a = keep.tile([P, HEAD], F32)
@@ -158,7 +156,7 @@ def tile_picked_canddetminmx_none_po_kernel(
         z_late = keep.tile([P, BLOCK * PACK], BF16, align_bytes=64, tag="z_late")
         z_block = [z_early[:, : BLOCK * PACK], z_early[:, BLOCK * PACK :], z_late[:]]
         for b in range(blocks):
-            pairs = keep.tile([P, 2, P, 2], BF16, name="pairs%d" % b)
+            pairs = keep.tile([P, 2, P, 2], BF16, name="pairs%d" % b, tag="pairs%d" % (b % 2))
             nc.scalar.copy(pairs[:], turned[b][:].rearrange("j (u e) p -> j u p e", e=2))
             back = psum.tile([P, 2, BLOCK], F32, name="back%d" % b, tag="turned%d" % b)
             words = pairs[:].rearrange("j u p e -> j (u p e)").bitcast(F32)
@@ -179,12 +177,15 @@ def tile_picked_canddetminmx_none_po_kernel(
             products(t, HEAD, S, tail_first[:, t, :], tail_second[:, t, :], factor_a[:, cols], factor_c[:, cols])
         quantize_z(z_early[:], 0, EARLY)
         score(0, EARLY)
-        leave(0, EARLY)
-        for t in range(2):
-            nc.scalar.activation(s_plain[t][:, :EARLY], s_bank[t][:, :EARLY], COPY, scale=0.0625)
+        leave(s_win[0], s_bank[0], 0, EARLY)
+        leave(s_win[1], s_bank[1], 0, EARLY)
+        leave(s_win[2], s_bank[2], 0, EARLY)
+        leave(s_win[3], s_bank[3], 0, EARLY)
         last = keep.tile([P, 2, BLOCK], F32, align_bytes=64, tag="z_early")
         products(PACK - 1, HEAD, S, tail_first[:, PACK - 1, :], tail_second[:, PACK - 1, :], last[:, 0, :], last[:, 1, :])
         quantize_z(z_late[:], EARLY, HEAD)
+        score(EARLY, HEAD, (0,))
+        leave(s_win[0], s_bank[0], EARLY, HEAD)
         z_tail = keep.tile([P, (S - HEAD) * PACK], BF16, align_bytes=64, tag="z_late")
         nc.vector.tensor_tensor(
             z_tail[:].rearrange("p (c i t) -> p c t i", i=2, t=PACK),
@@ -193,11 +194,12 @@ def tile_picked_canddetminmx_none_po_kernel(
             ALU.add,
         )
         quantize_z(z_tail[:], HEAD, S)
-        score(EARLY, S)
-        for t in range(PACK):
-            nc.scalar.activation(s_win[t][:, EARLY:], s_bank[t][:, EARLY:], COPY, scale=0.0625)
-            lo = EARLY if t < 2 else 0
-            nc.scalar.activation(s_plain[t][:, lo:], s_bank[t][:, lo:], COPY, scale=0.0625)
+        last_bank = psum.tile([P, S], F32, tag="turned3")
+        score(HEAD, S, (0,), last_bank)
+        score(EARLY, S, range(1, PACK))
+        leave(s_win[0], last_bank, HEAD, S)
+        for t in range(1, PACK):
+            leave(s_win[t], s_bank[t], EARLY, S)
 
         out_rows = out_0.rearrange("(p t) j -> p t j", t=PACK)
         out_words = out_1[0].rearrange("p n r -> p (n r)").bitcast(I32)
@@ -216,13 +218,14 @@ def tile_picked_canddetminmx_none_po_kernel(
                 cols = slice(b * BLOCK, (b + 1) * BLOCK)
                 nc.tensor.matmul(across[t][:, b, :], s_win[t][:, cols], ident[:], start=b == 0, stop=False, is_transpose=True)
 
+        larger_tail = []
+        fetched = [keep.tile([P, S], F32, name="fetched%d" % t) for t in range(PACK)]
+
         def larger_of(t):
             excess = keep.tile([P, S], F32, name="excess%d" % t)
             for lo in (0, S // 2):
-                cols = slice(lo, lo + S // 2)
-                nc.vector.tensor_tensor(
-                    excess[:, cols], s_win[t][:].indirect(entries(n5_t, lo, lo + S // 2)), s_plain[t][:, cols], ALU.subtract
-                )
+                nc.vector.tensor_copy(fetched[t][:, lo : lo + S // 2], s_win[t][:].indirect(entries(n5_t, lo, lo + S // 2)))
+            nc.gpsimd.tensor_tensor(excess[:], fetched[t][:], s_win[t][:], ALU.subtract)
             rise = ring.tile([P, S], F32, name="rise")
             nc.scalar.activation(rise[:], excess[:], RELU)
             for b in range(PACK):
@@ -232,47 +235,44 @@ def tile_picked_canddetminmx_none_po_kernel(
                 )
             staged = ring.tile([P, PACK, BLOCK], F32, name="staged")
             nc.scalar.copy(staged[:], across[t][:])
-            larger = psum.tile([P, S], F32, name="larger%d" % t, tag="bank%d" % t)
-            for b in range(PACK):
+            larger = psum.tile([P, HEAD], F32, name="larger%d" % t, tag="bank%d" % t)
+            for b in range(blocks):
                 nc.tensor.transpose(larger[:, b * BLOCK : (b + 1) * BLOCK], staged[:, b, :], ident[:])
+            if t == 0:
+                larger_tail.append(psum.tile([P, PACK, BLOCK], F32, name="larger_tail", tag="turned0"))
+            nc.tensor.transpose(larger_tail[0][:, t, :], staged[:, blocks, :], ident[:])
             return larger
 
-        pieces = ((0, HEAD), (HEAD, S))
-        spare = keep.tile([P, HEAD], F32)
         result_head = keep.tile([P, PACK, HEAD], F32)
         result_tail = keep.tile([P, PACK, BLOCK], F32)
-        rounded = [keep.tile([P, (hi - lo) * PACK], BF16, name="rounded%d" % lo, align_bytes=64) for lo, hi in pieces]
-        got_head = [spare[:], s_plain[2][:, :HEAD], spare[:], s_plain[3][:, :HEAD]]
-        got_tail = [s_plain[2][:, :BLOCK]] + [s_plain[3][:, k * BLOCK : (k + 1) * BLOCK] for k in range(3)]
+        rounded = keep.tile([P, HEAD * PACK], BF16, align_bytes=64)
+        got_head = [fetched[k][:, :HEAD] for k in (1, 2, 3, 1)]
+        got_tail = fetched[1][:].rearrange("p (t j) -> p t j", t=PACK)
 
-        fetch(0, 0, HEAD, got_head[0])
         larger = [larger_of(t) for t in range(PACK)]
-        fetch(1, 0, HEAD, got_head[1])
+        for t in range(PACK - 1):
+            fetch(t, 0, HEAD, got_head[t])
         for t in range(PACK):
-            nc.vector.tensor_tensor(result_head[:, t, :], larger[t][:, :HEAD], got_head[t], ALU.min)
+            nc.vector.tensor_tensor(result_head[:, t, :], larger[t][:], got_head[t], ALU.min)
             nc.sync.dma_start(out_rows[:, t, :HEAD], result_head[:, t, :])
-            if t + 2 < PACK:
-                fetch(t + 2, 0, HEAD, got_head[t + 2])
+            if t == 0:
+                fetch(PACK - 1, 0, HEAD, got_head[PACK - 1])
         for a, b in ((0, EARLY), (EARLY, HEAD)):
             nc.scalar.copy(
-                rounded[0][:, a * PACK : b * PACK].rearrange("p (c i t) -> p c t i", i=2, t=PACK),
+                rounded[:, a * PACK : b * PACK].rearrange("p (c i t) -> p c t i", i=2, t=PACK),
                 result_head[:, :, a:b].rearrange("p t (c i) -> p c t i", i=2),
             )
-        fetch(0, HEAD, S, got_tail[0])
         for t in range(PACK):
-            if t + 1 < PACK:
-                fetch(t + 1, HEAD, S, got_tail[t + 1])
-            else:
-                quantize_out(rounded[0][:, : EARLY * PACK], 0, EARLY)
-            nc.vector.tensor_tensor(result_tail[:, t, :], larger[t][:, HEAD:], got_tail[t], ALU.min)
-            if t % 2:
-                nc.sync.dma_start(out_rows[:, t - 1 : t + 1, HEAD:], result_tail[:, t - 1 : t + 1, :])
+            fetch(t, HEAD, S, got_tail[:, t, :])
+        nc.vector.tensor_tensor(result_tail[:], larger_tail[0][:], got_tail, ALU.min)
+        nc.sync.dma_start(out_rows[:, :, HEAD:], result_tail[:])
+        quantize_out(rounded[:, : EARLY * PACK], 0, EARLY)
         nc.vector.tensor_copy(
-            rounded[1][:].rearrange("p (c i t) -> p c t i", i=2, t=PACK),
+            rounded[:, : BLOCK * PACK].rearrange("p (c i t) -> p c t i", i=2, t=PACK),
             result_tail[:].rearrange("p t (c i) -> p c t i", i=2),
         )
-        quantize_out(rounded[0][:, EARLY * PACK :], EARLY, HEAD)
-        quantize_out(rounded[1][:], HEAD, S)
+        quantize_out(rounded[:, EARLY * PACK :], EARLY, HEAD)
+        quantize_out(rounded[:, : BLOCK * PACK], HEAD, S)
         nc.sync.dma_start(out_words[:, :EARLY], o_codes[:, :EARLY])
         nc.sync.dma_start(out_words[:, EARLY:], o_codes[:, EARLY:])
         for q in range(4):

from contextlib import ExitStack

import concourse.mybir as mybir
from concourse.masks import make_identity

F32 = mybir.dt.float32
BF16 = mybir.dt.bfloat16
I32 = mybir.dt.int32
U32 = mybir.dt.uint32
U16 = mybir.dt.uint16
U8 = mybir.dt.uint8
FP8X4 = mybir.dt.float8_e4m3fn_x4
FP4X4 = mybir.dt.float4_e2m1fn_x4
ALU = mybir.AluOpType
COPY = mybir.ActivationFunctionType.Copy
RELU = mybir.ActivationFunctionType.Relu

P = 128
PACK = 4
T = 2048
S = 512
BLOCK = 128
HEAD = 384
EARLY = 256
FLOPS = 2 * 2 * 512 * 512 * 512


def tile_picked_canddetminmx_none_po_kernel(
    tc, x_words, x_scales, w1_words, w1_scales, gs, offs, n1, n2, n3, n4, cand, n5, n6, out_0, out_1, out_2
):
    nc = tc.nc
    with ExitStack() as ctx:
        keep = ctx.enter_context(tc.tile_pool(name="keep", bufs=1))
        ring = ctx.enter_context(tc.tile_pool(name="ring", bufs=2))
        deep = ctx.enter_context(tc.tile_pool(name="deep", bufs=3))
        psum = ctx.enter_context(tc.psum_pool(name="psum", bufs=1))

        def load_list(name, src):
            tile = keep.tile([P, S // 16], U16, name=name)
            nc.sync.dma_start(tile[:], src)
            return tile

        def load_scale_rows(tile, src):
            for q in range(4):
                nc.sync.dma_start(tile[32 * q : 32 * q + 4, :].bitcast(I32), src[0, 4 * q : 4 * q + 4, :].bitcast(I32))

        def entries(lst, lo, hi):
            return lst[:, lo // 16 : hi // 16]

        x_plane = keep.tile([P, T], U8, align_bytes=64)
        w_plane = keep.tile([P, S], U8, align_bytes=64, tag="w_plane")
        nc.gpsimd.memset(x_plane[:].bitcast(I32), 0)
        nc.gpsimd.memset(w_plane[:].bitcast(I32), 0)

        offs_t = load_list("offs_t", offs)
        load_scale_rows(x_plane, x_scales)
        cand_t = load_list("cand_t", cand)
        w_raw = keep.tile([P, 2 * S], U8, align_bytes=64)
        nc.sync.dma_start(w_raw[:].bitcast(I32), w1_words[0].bitcast(I32))
        x_table = keep.tile([P, T], I32, align_bytes=64)
        nc.sync.dma_start(x_table[:], x_words[0].rearrange("p n r -> p (n r)").bitcast(I32))
        load_scale_rows(w_plane, w1_scales)
        gain = keep.tile([P, PACK], F32)
        nc.sync.dma_start(gain[:], gs.rearrange("(p t) o -> p (t o)", t=PACK))
        n1_t = load_list("n1_t", n1)
        n3_t = load_list("n3_t", n3)
        n2_t = load_list("n2_t", n2)
        n4_t = load_list("n4_t", n4)
        n5_t = load_list("n5_t", n5)
        n6_t = load_list("n6_t", n6)

        ident = keep.tile([P, P], F32)
        make_identity(nc, ident[:])

        xq_scales = keep.tile([P, S], U8, align_bytes=64)
        nc.vector.tensor_copy(xq_scales[:], x_plane[:].indirect(offs_t[:]))
        cand_scales_raw = keep.tile([P, S], U8, align_bytes=64)
        nc.vector.tensor_copy(cand_scales_raw[:], x_plane[:].indirect(cand_t[:]))
        w_codes = [keep.tile([P, BLOCK, 2], U8, align_bytes=64, name="w_codes%d" % t) for t in range(PACK)]
        w_scales = [keep.tile([P, BLOCK], U8, align_bytes=64, name="w_scales%d" % t) for t in range(PACK)]
        for t in range(PACK):
            nc.gpsimd.tensor_copy(w_codes[t][:], w_raw[:].rearrange("p (m t b) -> p t m b", t=PACK, b=2)[:, t, :, :])
            nc.gpsimd.tensor_copy(w_scales[t][:], w_plane[:].rearrange("p (m t) -> p t m", t=PACK)[:, t, :])
        xq_codes = keep.tile([P, S], U32, align_bytes=64)
        for lo in (0, S // 2):
            nc.vector.tensor_copy(
                xq_codes[:, lo : lo + S // 2], x_table[:].bitcast(U32).indirect(entries(offs_t, lo, lo + S // 2))
            )
        cand_codes = keep.tile([P, PACK, BLOCK], U32, align_bytes=64)
        nc.vector.tensor_copy(cand_codes[:].rearrange("p t m -> p m t"), x_table[:].bitcast(U32).indirect(cand_t[:]))
        cand_scales = keep.tile([P, PACK, BLOCK], U8, align_bytes=64)
        nc.vector.tensor_copy(cand_scales[:], cand_scales_raw[:].rearrange("p (m t) -> p t m", t=PACK))

        y_gain = [keep.tile([P, S], F32, name="y_gain%d" % t) for t in range(PACK)]
        y_pos = [keep.tile([P, S], F32, name="y_pos%d" % t) for t in range(PACK)]
        y_neg = [keep.tile([P, S], F32, name="y_neg%d" % t) for t in range(PACK)]
        for t in range(PACK):
            parts = ((0, S // 2, "turned3"), (S // 2, S, "bank0")) if t == 0 else ((0, S, "bank%d" % t),)
            banks = []
            for lo, hi, tag in parts:
                bank = psum.tile([P, hi - lo], F32, name="y_bank", tag=tag)
                banks.append(bank)
                nc.tensor.matmul_mx(
                    out=bank[:],
                    lhsT=w_codes[t][:].rearrange("p m b -> p (m b)").bitcast(FP4X4),
                    lhsT_scale=w_scales[t][:],
                    rhs=xq_codes[:, lo:hi].bitcast(FP8X4),
                    rhs_scale=xq_scales[:, lo:hi],
                    start=True,
                    stop=True,
                )
            for window, scale in ((y_pos[t], 0.75), (y_neg[t], -0.75), (y_gain[t], gain[:, t : t + 1])):
                for (lo, hi, tag), bank in zip(parts, banks):
                    nc.scalar.activation(window[:, lo:hi], bank[:], COPY, scale=scale)

        z_codes = keep.tile([P, S], U32, align_bytes=64)
        z_scales = keep.tile([P, S], U8, align_bytes=64)
        s_bank = [psum.tile([P, S], F32, name="s_bank%d" % t, tag="bank%d" % t) for t in range(PACK)]
        s_win = [keep.tile([P, S], F32, name="s_win%d" % t) for t in range(PACK)]


        def products(t, lo, hi, first, second, a, c):
            nc.vector.tensor_copy(a, y_pos[t][:].indirect(entries(n1_t, lo, hi)))
            nc.vector.tensor_copy(c, y_neg[t][:].indirect(entries(n3_t, lo, hi)))
            nc.vector.tensor_tensor(first, y_gain[t][:].indirect(entries(n2_t, lo, hi)), a, ALU.mult)
            nc.vector.tensor_tensor(second, y_gain[t][:].indirect(entries(n4_t, lo, hi)), c, ALU.mult)

        def score(lo, hi, tiles=range(PACK), bank=None):
            for t in tiles:
                nc.tensor.matmul_mx(
                    out=(s_bank[t] if bank is None else bank)[:, lo:hi],
                    lhsT=cand_codes[:, t, :].bitcast(FP8X4),
                    lhsT_scale=cand_scales[:, t, :],
                    rhs=z_codes[:, lo:hi].bitcast(FP8X4),
                    rhs_scale=z_scales[:, lo:hi],
                    start=True,
                    stop=True,
                )

        def leave(tile, bank, lo, hi):
            nc.scalar.activation(tile[:, lo:hi], bank[:, lo:hi], COPY, scale=0.0625)

        blocks = HEAD // BLOCK
        factor_a = keep.tile([P, HEAD], F32)
        factor_c = keep.tile([P, HEAD], F32)
        turned = [psum.tile([P, PACK, BLOCK], F32, name="turned%d" % b) for b in range(blocks)]
        for t in range(PACK):
            first = ring.tile([P, HEAD], F32, name="first")
            second = ring.tile([P, HEAD], F32, name="second")
            products(t, 0, HEAD, first[:], second[:], factor_a[:], factor_c[:])
            for b in range(blocks):
                cols = slice(b * BLOCK, (b + 1) * BLOCK)
                nc.tensor.matmul(turned[b][:, t, :], first[:, cols], ident[:], start=True, stop=False, is_transpose=True)
                nc.tensor.matmul(turned[b][:, t, :], second[:, cols], ident[:], start=False, stop=True, is_transpose=True)
        z_early = keep.tile([P, EARLY * PACK], BF16, align_bytes=64, tag="z_early")
        z_late = keep.tile([P, BLOCK * PACK], BF16, align_bytes=64, tag="z_late")
        z_block = [z_early[:, : BLOCK * PACK], z_early[:, BLOCK * PACK :], z_late[:]]
        for b in range(blocks):
            pairs = keep.tile([P, 2, P, 2], BF16, name="pairs%d" % b, tag="pairs%d" % (b % 2))
            nc.scalar.copy(pairs[:], turned[b][:].rearrange("j (u e) p -> j u p e", e=2))
            back = psum.tile([P, 2, BLOCK], F32, name="back%d" % b, tag="turned%d" % b)
            words = pairs[:].rearrange("j u p e -> j (u p e)").bitcast(F32)
            for u in range(2):
                nc.tensor.transpose(back[:, u, :], words[:, u * P : (u + 1) * P], ident[:])
            nc.scalar.copy(
                z_block[b].bitcast(F32).rearrange("p (j u) -> p j u", u=2),
                back[:].rearrange("p u j -> p j u"),
            )

        def quantize_z(src, lo, hi):
            nc.vector.quantize_mx(out=z_codes[:, lo:hi].bitcast(FP8X4), scales=z_scales[:, lo:hi], in_=src)

        tail_first = keep.tile([P, PACK, S - HEAD], F32)
        tail_second = keep.tile([P, PACK, S - HEAD], F32)
        for t in range(PACK - 1):
            cols = slice(t * BLOCK, (t + 1) * BLOCK)
            products(t, HEAD, S, tail_first[:, t, :], tail_second[:, t, :], factor_a[:, cols], factor_c[:, cols])
        quantize_z(z_early[:], 0, EARLY)
        score(0, EARLY)
        leave(s_win[0], s_bank[0], 0, EARLY)
        leave(s_win[1], s_bank[1], 0, EARLY)
        leave(s_win[2], s_bank[2], 0, EARLY)
        leave(s_win[3], s_bank[3], 0, EARLY)
        last = keep.tile([P, 2, BLOCK], F32, align_bytes=64, tag="z_early")
        products(PACK - 1, HEAD, S, tail_first[:, PACK - 1, :], tail_second[:, PACK - 1, :], last[:, 0, :], last[:, 1, :])
        quantize_z(z_late[:], EARLY, HEAD)
        score(EARLY, HEAD, (0,))
        leave(s_win[0], s_bank[0], EARLY, HEAD)
        z_tail = keep.tile([P, (S - HEAD) * PACK], BF16, align_bytes=64, tag="z_late")
        nc.vector.tensor_tensor(
            z_tail[:].rearrange("p (c i t) -> p c t i", i=2, t=PACK),
            tail_first[:].rearrange("p t (c i) -> p c t i", i=2),
            tail_second[:].rearrange("p t (c i) -> p c t i", i=2),
            ALU.add,
        )
        quantize_z(z_tail[:], HEAD, S)
        last_bank = psum.tile([P, S], F32, tag="turned3")
        score(HEAD, S, (0,), last_bank)
        score(EARLY, S, range(1, PACK))
        leave(s_win[0], last_bank, HEAD, S)
        for t in range(1, PACK):
            leave(s_win[t], s_bank[t], EARLY, S)

        out_rows = out_0.rearrange("(p t) j -> p t j", t=PACK)
        out_words = out_1[0].rearrange("p n r -> p (n r)").bitcast(I32)
        o_codes = keep.tile([P, S], I32, align_bytes=64)
        o_scales = keep.tile([P, S], U8, align_bytes=64)

        def quantize_out(src, lo, hi):
            nc.vector.quantize_mx(out=o_codes[:, lo:hi].bitcast(FP8X4), scales=o_scales[:, lo:hi], in_=src)

        def fetch(t, lo, hi, got):
            nc.vector.tensor_copy(got, s_win[t][:].indirect(entries(n6_t, lo, hi)))

        across = [psum.tile([P, PACK, BLOCK], F32, name="across%d" % t, tag="turned%d" % t) for t in range(PACK)]
        for t in range(PACK):
            for b in range(PACK):
                cols = slice(b * BLOCK, (b + 1) * BLOCK)
                nc.tensor.matmul(across[t][:, b, :], s_win[t][:, cols], ident[:], start=b == 0, stop=False, is_transpose=True)

        larger_tail = []
        fetched = [keep.tile([P, S], F32, name="fetched%d" % t) for t in range(PACK)]

        def larger_of(t):
            excess = keep.tile([P, S], F32, name="excess%d" % t)
            for lo in (0, S // 2):
                nc.vector.tensor_copy(fetched[t][:, lo : lo + S // 2], s_win[t][:].indirect(entries(n5_t, lo, lo + S // 2)))
            nc.gpsimd.tensor_tensor(excess[:], fetched[t][:], s_win[t][:], ALU.subtract)
            rise = ring.tile([P, S], F32, name="rise")
            nc.scalar.activation(rise[:], excess[:], RELU)
            for b in range(PACK):
                cols = slice(b * BLOCK, (b + 1) * BLOCK)
                nc.tensor.matmul(
                    across[t][:, b, :], rise[:, cols], ident[:], start=False, stop=b == PACK - 1, is_transpose=True
                )
            staged = ring.tile([P, PACK, BLOCK], F32, name="staged")
            nc.scalar.copy(staged[:], across[t][:])
            larger = psum.tile([P, HEAD], F32, name="larger%d" % t, tag="bank%d" % t)
            for b in range(blocks):
                nc.tensor.transpose(larger[:, b * BLOCK : (b + 1) * BLOCK], staged[:, b, :], ident[:])
            if t == 0:
                larger_tail.append(psum.tile([P, PACK, BLOCK], F32, name="larger_tail", tag="turned0"))
            nc.tensor.transpose(larger_tail[0][:, t, :], staged[:, blocks, :], ident[:])
            return larger

        result_head = keep.tile([P, PACK, HEAD], F32)
        result_tail = keep.tile([P, PACK, BLOCK], F32)
        rounded = keep.tile([P, HEAD * PACK], BF16, align_bytes=64)
        got_head = [fetched[k][:, :HEAD] for k in (1, 2, 3, 1)]
        got_tail = fetched[1][:].rearrange("p (t j) -> p t j", t=PACK)

        larger = [larger_of(t) for t in range(PACK)]
        for t in range(PACK - 1):
            fetch(t, 0, HEAD, got_head[t])
        for t in range(PACK):
            nc.vector.tensor_tensor(result_head[:, t, :], larger[t][:], got_head[t], ALU.min)
            nc.sync.dma_start(out_rows[:, t, :HEAD], result_head[:, t, :])
            if t == 0:
                fetch(PACK - 1, 0, HEAD, got_head[PACK - 1])
        for a, b in ((0, EARLY), (EARLY, HEAD)):
            nc.scalar.copy(
                rounded[:, a * PACK : b * PACK].rearrange("p (c i t) -> p c t i", i=2, t=PACK),
                result_head[:, :, a:b].rearrange("p t (c i) -> p c t i", i=2),
            )
        for t in range(PACK):
            fetch(t, HEAD, S, got_tail[:, t, :])
        nc.vector.tensor_tensor(result_tail[:], larger_tail[0][:], got_tail, ALU.min)
        nc.sync.dma_start(out_rows[:, :, HEAD:], result_tail[:])
        quantize_out(rounded[:, : EARLY * PACK], 0, EARLY)
        nc.vector.tensor_copy(
            rounded[:, : BLOCK * PACK].rearrange("p (c i t) -> p c t i", i=2, t=PACK),
            result_tail[:].rearrange("p t (c i) -> p c t i", i=2),
        )
        quantize_out(rounded[:, EARLY * PACK :], EARLY, HEAD)
        quantize_out(rounded[:, : BLOCK * PACK], HEAD, S)
        nc.sync.dma_start(out_words[:, :EARLY], o_codes[:, :EARLY])
        nc.sync.dma_start(out_words[:, EARLY:], o_codes[:, EARLY:])
        for q in range(4):
            queue = nc.scalar if q % 2 else nc.sync
            queue.dma_start(out_2[0, 4 * q : 4 * q + 4, :].bitcast(I32), o_scales[32 * q : 32 * q + 4, :].bitcast(I32))
